import numpy as np
import ml_dtypes


def mxq(x, axis, fmt="e4m3"):
    dtype, down = {"e4m3": (ml_dtypes.float8_e4m3fn, 7), "e5m2": (ml_dtypes.float8_e5m2, 14)}[fmt]
    v = np.moveaxis(np.asarray(x, np.float32).astype(ml_dtypes.bfloat16).astype(np.float64), axis, -1)
    blocks = v.reshape(v.shape[:-1] + (-1, 32))
    amax = np.abs(blocks).max(-1, keepdims=True)
    byte = np.maximum(np.where(amax > 0, np.frexp(amax)[1] - 1 + 127, 0) - down, 1)
    scale = np.exp2(byte - 127.0)
    codes = (blocks / scale).astype(np.float32).astype(dtype).astype(np.float64)
    return np.moveaxis((codes * scale).reshape(v.shape), -1, axis)


WIDE = False


def mx_kscale(k):
    if not WIDE:
        return np.ones(k)
    levels = np.array([10, -10, 5, -5, 0])
    if k % 512:
        return np.exp2(np.random.permutation(np.resize(levels, k // 32))).repeat(32)
    a = np.empty((k // 512, 16))
    for p in range(k // 512):
        a[p, :8] = np.random.permutation(np.resize(levels, 8))
        for g in range(8):
            far = levels[np.abs(levels - a[p, g]) >= 10]
            a[p, g + 8] = far[np.random.randint(len(far))]
    return np.exp2(a.ravel()).repeat(32)


def f64(x):
    return np.asarray(x).astype(np.float64)


def striped(idx):
    return np.tile(np.asarray(idx).reshape(-1, 16).T, (8, 1)).astype(np.uint16)


def unstriped(offs):
    return offs[:16].T.reshape(-1).astype(np.int64)


E2M1 = np.array([0.0, 0.5, 1.0, 1.5, 2.0, 3.0, 4.0, 6.0, -0.0, -0.5, -1.0, -1.5, -2.0, -3.0, -4.0, -6.0])


def pack_weight(w, fmt):
    k, n = w.shape
    w = f64(np.asarray(w, np.float32).astype(ml_dtypes.bfloat16)).reshape(k // 32, 32, n)
    amax = np.abs(w).max(1)
    if fmt == "e4m3":
        byte = np.frexp(amax)[1] - 1 + 127 - 7
    else:
        mant, ex = np.frexp(amax / 6.0)
        byte = np.where(mant > 0.5, ex, ex - 1) + 127
    byte = np.clip(np.where(amax > 0, byte, 1), 1, 254)
    scaled = (w * np.exp2(127.0 - byte)[:, None, :]).reshape(k, n).astype(np.float32)
    by_word = np.ascontiguousarray(scaled.reshape(k // 512, 128, 4, n).transpose(0, 1, 3, 2))
    if fmt == "e4m3":
        words = by_word.astype(ml_dtypes.float8_e4m3fn).view(np.uint8)
    else:
        c = by_word.astype(ml_dtypes.float4_e2m1fn).view(np.uint8) & 0xF
        words = (c[..., 0::2] | (c[..., 1::2] << 4)).reshape(k // 512, 128, 2 * n)
    return np.ascontiguousarray(words), np.ascontiguousarray(byte.astype(np.uint8).reshape(k // 512, 16, n))


def unpack_weight(words, scales, fmt):
    g, _, n = scales.shape
    words = np.ascontiguousarray(words).reshape(g, 128, n, -1)
    if fmt == "e4m3":
        vals = words.view(ml_dtypes.float8_e4m3fn).astype(np.float64)
    else:
        nib = np.empty((g, 128, n, 4), np.uint8)
        nib[..., 0::2] = words & 0xF
        nib[..., 1::2] = words >> 4
        vals = E2M1[nib]
    vals = vals * np.repeat(np.exp2(scales.astype(np.float64) - 127.0), 8, axis=1)[..., None]
    return vals.transpose(0, 1, 3, 2).reshape(g * 512, n)


def sigmoid(v):
    return 1.0 / (1.0 + np.exp(-v))


D, T, I, Q, E = 512, 2048, 512, 128, 512


def setup_inputs():
    n = np.random.standard_normal
    idx = np.random.permutation(T)[:I]
    fd = mx_kscale(D)
    fi = mx_kscale(I)
    ti = np.ones(T)
    ti[idx] = fi
    keysp = pack_weight(n((D, T)) / fd[:, None], "e2m1")
    return {
        "query": (n((D, Q)) * 0.4 / np.sqrt(D) * fd[:, None]).astype(np.float32),
        "keys_words": keysp[0],
        "keys_scales": keysp[1],
        "th": (np.random.uniform(0.8, 1.6, (Q, 1))).astype(np.float32),
        "steep": (np.random.uniform(1.0, 4.0, (Q, 1))).astype(np.float32),
        "kept": (n((Q, E)) * 0.08).astype(np.float32),
        "size": (np.random.uniform(0.5, 2.0, (1, I)) * fi).astype(np.float32),
        "vals": (n((E, T)) / ti).astype(np.float32),
        "offs": striped(idx),
    }


def reference(query, keys_words, keys_scales, th, steep, kept, size, vals, offs):
    idx = unstriped(offs)
    keysu = unpack_weight(keys_words, keys_scales, "e2m1")
    queryq = mxq(f64(query), 0, "e4m3")
    keysidxg = keysu[:, idx]
    a = queryq.T @ keysidxg
    z = np.max(a, axis=1, keepdims=True)
    g = sigmoid(f64(steep) * (z - f64(th)))
    p = np.exp(a - z)
    w = p * f64(size) / np.sum(p, axis=1, keepdims=True)
    wt = w.T
    vt = f64(vals)[:, idx].T
    wtq = mxq(wt, 0, "e4m3")
    vtq = mxq(vt, 0, "e4m3")
    o = wtq.T @ vtq
    y = f64(kept) + (o - f64(kept)) * g
    return y

@@ -1,0 +1,186 @@
+from contextlib import ExitStack
+
+import concourse.mybir as mybir
+from concourse.masks import make_identity
+
+F32 = mybir.dt.float32
+BF16 = mybir.dt.bfloat16
+I32 = mybir.dt.int32
+U32 = mybir.dt.uint32
+U16 = mybir.dt.uint16
+U8 = mybir.dt.uint8
+FP8X4 = mybir.dt.float8_e4m3fn_x4
+FP4X4 = mybir.dt.float4_e2m1fn_x4
+ALU = mybir.AluOpType
+ACT = mybir.ActivationFunctionType
+AX = mybir.AxisListType
+
+P = 128
+D, T, SLOTS, Q, E = 512, 2048, 512, 128, 512
+PACK = 4
+BLOCKS = E // P
+FLOPS = 2 * Q * SLOTS * D + 2 * Q * SLOTS * E
+
+
+def tile_attend_updateread_kernel(tc, query, keys_words, keys_scales, th, steep, kept, size, vals, offs, out):
+    nc = tc.nc
+    with ExitStack() as ctx:
+        sb = ctx.enter_context(tc.tile_pool(name="sb", bufs=1))
+        ps = ctx.enter_context(tc.psum_pool(name="ps", bufs=1))
+        ps_turn = ctx.enter_context(tc.psum_pool(name="ps_turn", bufs=2))
+
+        offsets = sb.tile([P, SLOTS // 16], U16, name="offsets")
+        key_words = sb.tile([P, T], U16, name="key_words", align_bytes=64)
+        key_bytes = sb.tile([P, T], U8, name="key_bytes", align_bytes=64)
+        query_raw = sb.tile([P, PACK, Q], F32, name="query_raw", align_bytes=64)
+        val_pool = [sb.tile([P, T], F32, name="val_pool%d" % b, align_bytes=64) for b in range(BLOCKS)]
+        kept_sb = sb.tile([P, E], F32, name="kept_sb", align_bytes=64)
+        th_sb = sb.tile([P, 1], F32, name="th_sb")
+        steep_sb = sb.tile([P, 1], F32, name="steep_sb")
+        size_sb = sb.tile([P, PACK], F32, name="size_sb")
+        ident = sb.tile([P, P], F32, name="ident", align_bytes=64)
+
+        nc.vector.memset(key_bytes[:].bitcast(I32), 0)
+        nc.sync.dma_start(offsets[:], offs)
+        nc.sync.dma_start(key_words[:].bitcast(I32), keys_words[0].bitcast(I32))
+        for quad in range(4):
+            nc.scalar.dma_start(
+                key_bytes[32 * quad : 32 * quad + 4, :].bitcast(I32),
+                keys_scales[0, 4 * quad : 4 * quad + 4, :].bitcast(I32),
+            )
+        nc.sync.dma_start(query_raw[:], query.rearrange("(p j) q -> p j q", j=PACK))
+        for b in range(BLOCKS):
+            nc.sync.dma_start(val_pool[b][:], vals[b * P : (b + 1) * P, :])
+        nc.sync.dma_start(kept_sb[:], kept)
+        nc.gpsimd.dma_start(size_sb[:], size.rearrange("o (p t) -> (o p) t", t=PACK))
+        nc.gpsimd.dma_start(steep_sb[:], steep)
+        nc.gpsimd.dma_start(th_sb[:], th)
+        make_identity(nc, ident[:])
+
+        def quantise(name, grouped):
+            codes = sb.tile([P, P], U32, name=name + "_codes", align_bytes=64)
+            scales = sb.tile([P, P], U8, name=name + "_scales", align_bytes=64)
+            nc.vector.quantize_mx(out=codes[:].bitcast(FP8X4), scales=scales[:], in_=grouped[:])
+            return codes, scales
+
+        def turn(name, rows):
+            words = rows[:].bitcast(F32)
+            turned = ps_turn.tile([P, 2, P], F32, name="turned")
+            for u in range(2):
+                nc.tensor.transpose(turned[:, u, :], words[:, u : SLOTS // 2 : 2], ident[:])
+            grouped = sb.tile([P, P * PACK], BF16, name=name + "_grouped", align_bytes=64)
+            nc.scalar.copy(
+                grouped[:].bitcast(F32).rearrange("p (c u) -> p c u", u=2),
+                turned[:].rearrange("p u c -> p c u"),
+            )
+            return grouped
+
+        def gather_values(b):
+            picked = sb.tile([P, SLOTS], BF16, name="val_picked%d" % b, align_bytes=64)
+            nc.vector.tensor_copy(picked[:], val_pool[b][:].indirect(offsets[:]))
+            return picked
+
+        key_words_picked = sb.tile([P, SLOTS], U16, name="key_words_picked", align_bytes=64)
+        key_bytes_picked = sb.tile([P, SLOTS], U8, name="key_bytes_picked", align_bytes=64)
+        nc.vector.tensor_copy(key_words_picked[:], key_words[:].indirect(offsets[:]))
+        nc.vector.tensor_copy(key_bytes_picked[:], key_bytes[:].indirect(offsets[:]))
+
+        query_grouped = sb.tile([P, Q * PACK], BF16, name="query_grouped", align_bytes=64)
+        nc.scalar.copy(
+            query_grouped[:].rearrange("p (q j) -> p q j", j=PACK),
+            query_raw[:].rearrange("p j q -> p q j"),
+        )
+        query_codes, query_scales = quantise("query", query_grouped)
+
+        scores = ps.tile([P, SLOTS], F32, name="scores")
+        nc.tensor.matmul_mx(
+            out=scores[:],
+            lhsT=query_codes[:].bitcast(FP8X4),
+            lhsT_scale=query_scales[:],
+            rhs=key_words_picked[:].bitcast(FP4X4),
+            rhs_scale=key_bytes_picked[:],
+            start=True,
+            stop=True,
+        )
+
+        size_rows = ps.tile([P, PACK, P], F32, name="size_rows")
+        for t in range(PACK):
+            nc.tensor.transpose(size_rows[:, t, :], size_sb[:, t : t + 1].to_broadcast([P, P]), ident[:])
+
+        gate_scale = sb.tile([P, 1], F32, name="gate_scale")
+        gate_bias = sb.tile([P, 1], F32, name="gate_bias")
+        nc.scalar.activation(gate_scale[:], steep_sb[:], ACT.Copy, scale=-0.5)
+        nc.scalar.activation(gate_bias[:], th_sb[:], ACT.Copy, scale=gate_scale[:])
+
+        picked0 = gather_values(0)
+
+        neg_best = sb.tile([P, 1], F32, name="neg_best")
+        nc.vector.tensor_reduce(neg_best[:], scores[:], AX.X, ALU.max, negate=True)
+        probs = sb.tile([P, SLOTS], F32, name="probs", align_bytes=64)
+        total = sb.tile([P, 1], F32, name="total")
+        nc.scalar.activation(probs[:], scores[:], ACT.Exp, bias=neg_best[:], accum_out=total[:])
+        half_swing = sb.tile([P, 1], F32, name="half_swing")
+        gate = sb.tile([P, 1], F32, name="gate")
+        keep = sb.tile([P, 1], F32, name="keep")
+        nc.scalar.activation(half_swing[:], neg_best[:], ACT.Tanh, bias=gate_bias[:], scale=gate_scale[:])
+        nc.scalar.activation(gate[:], half_swing[:], ACT.Copy, bias=0.5, scale=0.5)
+        nc.scalar.activation(keep[:], half_swing[:], ACT.Copy, bias=0.5, scale=-0.5)
+
+        grouped0 = turn("val0", picked0)
+        picked1 = gather_values(1)
+
+        inv_total = sb.tile([P, 1], F32, name="inv_total")
+        nc.vector.reciprocal(inv_total[:], total[:])
+        val_q = [quantise("val0", grouped0)]
+        weights = sb.tile([P, SLOTS], BF16, name="weights", align_bytes=64)
+        nc.vector.scalar_tensor_tensor(
+            weights[:].rearrange("p (s t) -> p s t", t=PACK),
+            probs[:].rearrange("p (s t) -> p s t", t=PACK),
+            inv_total[:],
+            size_rows[:].rearrange("p t s -> p s t"),
+            ALU.mult,
+            ALU.mult,
+        )
+        grouped1 = turn("val1", picked1)
+        weights_grouped = turn("weights", weights)
+        val_q.append(quantise("val1", grouped1))
+        picked2 = gather_values(2)
+        w_codes, w_scales = quantise("weights", weights_grouped)
+        grouped2 = turn("val2", picked2)
+        val_q.append(quantise("val2", grouped2))
+        picked3 = gather_values(3)
+
+        def read(bank, b):
+            nc.tensor.matmul_mx(
+                out=bank,
+                lhsT=w_codes[:].bitcast(FP8X4),
+                lhsT_scale=w_scales[:],
+                rhs=val_q[b][0][:].bitcast(FP8X4),
+                rhs_scale=val_q[b][1][:],
+                start=True,
+                stop=True,
+            )
+
+        early = (BLOCKS - 1) * P
+        read_early = ps.tile([P, early], F32, name="read_early")
+        for b in range(BLOCKS - 1):
+            read(read_early[:, b * P : (b + 1) * P], b)
+
+        kept_part = sb.tile([P, E], F32, name="kept_part", align_bytes=64)
+        nc.scalar.activation(kept_part[:], kept_sb[:], ACT.Copy, scale=keep[:])
+
+        grouped3 = turn("val3", picked3)
+        result_early = sb.tile([P, early], F32, name="result_early", align_bytes=64)
+        nc.vector.scalar_tensor_tensor(
+            result_early[:], read_early[:], gate[:], kept_part[:, 0:early], ALU.mult, ALU.add
+        )
+        nc.sync.dma_start(out[:, 0:early], result_early[:])
+
+        val_q.append(quantise("val3", grouped3))
+        read_late = ps.tile([P, P], F32, name="read_late")
+        read(read_late[:], BLOCKS - 1)
+        result_late = sb.tile([P, P], F32, name="result_late", align_bytes=64)
+        nc.vector.scalar_tensor_tensor(
+            result_late[:], read_late[:], gate[:], kept_part[:, early:E], ALU.mult, ALU.add
+        )
+        nc.sync.dma_start(out[:, early:E], result_late[:])

@@ -19,6 +19,7 @@ P = 128
 D, T, SLOTS, Q, E = 512, 2048, 512, 128, 512
 PACK = 4
 BLOCKS = E // P
+POOL_BYTES = 4 * T
 FLOPS = 2 * Q * SLOTS * D + 2 * Q * SLOTS * E
 
 
@@ -26,6 +27,7 @@ def tile_attend_updateread_kernel(tc, query, keys_words, keys_scales, th, steep,
     nc = tc.nc
     with ExitStack() as ctx:
         sb = ctx.enter_context(tc.tile_pool(name="sb", bufs=1))
+        vp = ctx.enter_context(tc.tile_pool(name="vp", bufs=1))
         ps = ctx.enter_context(tc.psum_pool(name="ps", bufs=1))
         ps_turn = ctx.enter_context(tc.psum_pool(name="ps_turn", bufs=2))
 
@@ -33,52 +35,53 @@ def tile_attend_updateread_kernel(tc, query, keys_words, keys_scales, th, steep,
         key_words = sb.tile([P, T], U16, name="key_words", align_bytes=64)
         key_bytes = sb.tile([P, T], U8, name="key_bytes", align_bytes=64)
         query_raw = sb.tile([P, PACK, Q], F32, name="query_raw", align_bytes=64)
-        val_pool = [sb.tile([P, T], F32, name="val_pool%d" % b, align_bytes=64) for b in range(BLOCKS)]
+        val_pool = [vp.tile([P, T], F32, name="val_pool%d" % b, offset=b * POOL_BYTES, align_bytes=64) for b in range(BLOCKS)]
         kept_sb = sb.tile([P, E], F32, name="kept_sb", align_bytes=64)
         th_sb = sb.tile([P, 1], F32, name="th_sb")
         steep_sb = sb.tile([P, 1], F32, name="steep_sb")
         size_sb = sb.tile([P, PACK], F32, name="size_sb")
         ident = sb.tile([P, P], F32, name="ident", align_bytes=64)
 
-        nc.vector.memset(key_bytes[:].bitcast(I32), 0)
+        nc.gpsimd.memset(key_bytes[:].bitcast(I32), 0)
         nc.sync.dma_start(offsets[:], offs)
         nc.sync.dma_start(key_words[:].bitcast(I32), keys_words[0].bitcast(I32))
         for quad in range(4):
-            nc.scalar.dma_start(
+            nc.sync.dma_start(
                 key_bytes[32 * quad : 32 * quad + 4, :].bitcast(I32),
                 keys_scales[0, 4 * quad : 4 * quad + 4, :].bitcast(I32),
             )
         nc.sync.dma_start(query_raw[:], query.rearrange("(p j) q -> p j q", j=PACK))
         for b in range(BLOCKS):
             nc.sync.dma_start(val_pool[b][:], vals[b * P : (b + 1) * P, :])
+            if b == 0:
+                nc.sync.dma_start(size_sb[:], size.rearrange("o (p t) -> (o p) t", t=PACK))
+                nc.sync.dma_start(steep_sb[:], steep)
+                nc.sync.dma_start(th_sb[:], th)
         nc.sync.dma_start(kept_sb[:], kept)
-        nc.gpsimd.dma_start(size_sb[:], size.rearrange("o (p t) -> (o p) t", t=PACK))
-        nc.gpsimd.dma_start(steep_sb[:], steep)
-        nc.gpsimd.dma_start(th_sb[:], th)
         make_identity(nc, ident[:])
 
-        def quantise(name, grouped):
-            codes = sb.tile([P, P], U32, name=name + "_codes", align_bytes=64)
-            scales = sb.tile([P, P], U8, name=name + "_scales", align_bytes=64)
-            nc.vector.quantize_mx(out=codes[:].bitcast(FP8X4), scales=scales[:], in_=grouped[:])
+        def after_gather(b, byte, shape, dtype, name):
+            return vp.tile(shape, dtype, name=name, offset=b * POOL_BYTES + byte, align_bytes=64)
+
+        def quantise(name, grouped, width, codes):
+            scales = sb.tile([P, width], U8, name=name + "_scales", align_bytes=64)
+            nc.vector.quantize_mx(out=codes[:].bitcast(FP8X4), scales=scales[:], in_=grouped)
             return codes, scales
 
-        def turn(name, rows):
-            words = rows[:].bitcast(F32)
+        def turn(rows, grouped):
+            words = rows.bitcast(F32)
             turned = ps_turn.tile([P, 2, P], F32, name="turned")
             for u in range(2):
                 nc.tensor.transpose(turned[:, u, :], words[:, u : SLOTS // 2 : 2], ident[:])
-            grouped = sb.tile([P, P * PACK], BF16, name=name + "_grouped", align_bytes=64)
             nc.scalar.copy(
-                grouped[:].bitcast(F32).rearrange("p (c u) -> p c u", u=2),
+                grouped.bitcast(F32).rearrange("p (c u) -> p c u", u=2),
                 turned[:].rearrange("p u c -> p c u"),
             )
-            return grouped
 
         def gather_values(b):
             picked = sb.tile([P, SLOTS], BF16, name="val_picked%d" % b, align_bytes=64)
             nc.vector.tensor_copy(picked[:], val_pool[b][:].indirect(offsets[:]))
-            return picked
+            return picked[:]
 
         key_words_picked = sb.tile([P, SLOTS], U16, name="key_words_picked", align_bytes=64)
         key_bytes_picked = sb.tile([P, SLOTS], U8, name="key_bytes_picked", align_bytes=64)
@@ -90,7 +93,9 @@ def tile_attend_updateread_kernel(tc, query, keys_words, keys_scales, th, steep,
             query_grouped[:].rearrange("p (q j) -> p q j", j=PACK),
             query_raw[:].rearrange("p j q -> p q j"),
         )
-        query_codes, query_scales = quantise("query", query_grouped)
+        query_codes, query_scales = quantise(
+            "query", query_grouped[:], Q, sb.tile([P, Q], U32, name="query_codes", align_bytes=64)
+        )
 
         scores = ps.tile([P, SLOTS], F32, name="scores")
         nc.tensor.matmul_mx(
@@ -114,11 +119,14 @@ def tile_attend_updateread_kernel(tc, query, keys_words, keys_scales, th, steep,
 
         picked0 = gather_values(0)
 
-        neg_best = sb.tile([P, 1], F32, name="neg_best")
+        neg_best = after_gather(0, 0, [P, 1], F32, "neg_best")
         nc.vector.tensor_reduce(neg_best[:], scores[:], AX.X, ALU.max, negate=True)
         probs = sb.tile([P, SLOTS], F32, name="probs", align_bytes=64)
         total = sb.tile([P, 1], F32, name="total")
         nc.scalar.activation(probs[:], scores[:], ACT.Exp, bias=neg_best[:], accum_out=total[:])
+
+        grouped0 = sb.tile([P, P * PACK], BF16, name="val_grouped0", align_bytes=64)
+        turn(picked0, grouped0[:])
         half_swing = sb.tile([P, 1], F32, name="half_swing")
         gate = sb.tile([P, 1], F32, name="gate")
         keep = sb.tile([P, 1], F32, name="keep")
@@ -126,12 +134,12 @@ def tile_attend_updateread_kernel(tc, query, keys_words, keys_scales, th, steep,
         nc.scalar.activation(gate[:], half_swing[:], ACT.Copy, bias=0.5, scale=0.5)
         nc.scalar.activation(keep[:], half_swing[:], ACT.Copy, bias=0.5, scale=-0.5)
 
-        grouped0 = turn("val0", picked0)
         picked1 = gather_values(1)
+        pair_grouped = sb.tile([P, 2 * P * PACK], BF16, name="pair_grouped", align_bytes=64)
+        turn(picked1, pair_grouped[:, P * PACK : 2 * P * PACK])
 
-        inv_total = sb.tile([P, 1], F32, name="inv_total")
+        inv_total = after_gather(1, 0, [P, 1], F32, "inv_total")
         nc.vector.reciprocal(inv_total[:], total[:])
-        val_q = [quantise("val0", grouped0)]
         weights = sb.tile([P, SLOTS], BF16, name="weights", align_bytes=64)
         nc.vector.scalar_tensor_tensor(
             weights[:].rearrange("p (s t) -> p s t", t=PACK),
@@ -141,46 +149,44 @@ def tile_attend_updateread_kernel(tc, query, keys_words, keys_scales, th, steep,
             ALU.mult,
             ALU.mult,
         )
-        grouped1 = turn("val1", picked1)
-        weights_grouped = turn("weights", weights)
-        val_q.append(quantise("val1", grouped1))
-        picked2 = gather_values(2)
-        w_codes, w_scales = quantise("weights", weights_grouped)
-        grouped2 = turn("val2", picked2)
-        val_q.append(quantise("val2", grouped2))
-        picked3 = gather_values(3)
+        turn(weights[:], pair_grouped[:, 0 : P * PACK])
+        codes0, scales0 = quantise("val0", grouped0[:], P, after_gather(1, 64, [P, P], U32, "val0_codes"))
 
-        def read(bank, b):
+        val_grouped = [None, None] + [
+            sb.tile([P, P * PACK], BF16, name="val_grouped%d" % b, align_bytes=64) for b in range(2, BLOCKS)
+        ]
+        turn(gather_values(2), val_grouped[2][:])
+        first_codes, first_scales = quantise("pair", pair_grouped[:], 2 * P, after_gather(2, 0, [P, 2 * P], U32, "pair_codes"))
+
+        def read(bank, codes, scales):
             nc.tensor.matmul_mx(
                 out=bank,
-                lhsT=w_codes[:].bitcast(FP8X4),
-                lhsT_scale=w_scales[:],
-                rhs=val_q[b][0][:].bitcast(FP8X4),
-                rhs_scale=val_q[b][1][:],
+                lhsT=first_codes[:, 0:P].bitcast(FP8X4),
+                lhsT_scale=first_scales[:, 0:P],
+                rhs=codes.bitcast(FP8X4),
+                rhs_scale=scales,
                 start=True,
                 stop=True,
             )
 
-        early = (BLOCKS - 1) * P
-        read_early = ps.tile([P, early], F32, name="read_early")
-        for b in range(BLOCKS - 1):
-            read(read_early[:, b * P : (b + 1) * P], b)
-
         kept_part = sb.tile([P, E], F32, name="kept_part", align_bytes=64)
+
+        def finish(name, bank, lo, hi):
+            result = sb.tile([P, hi - lo], F32, name=name, align_bytes=64)
+            nc.vector.scalar_tensor_tensor(result[:], bank, gate[:], kept_part[:, lo:hi], ALU.mult, ALU.add)
+            nc.sync.dma_start(out[:, lo:hi], result[:])
+
+        read01 = ps.tile([P, 2 * P], F32, name="read01")
+        read2 = ps.tile([P, P], F32, name="read2")
+        read3 = ps.tile([P, P], F32, name="read3")
+        read(read01[:, 0:P], codes0[:], scales0[:])
+        read(read01[:, P : 2 * P], first_codes[:, P : 2 * P], first_scales[:, P : 2 * P])
         nc.scalar.activation(kept_part[:], kept_sb[:], ACT.Copy, scale=keep[:])
-
-        grouped3 = turn("val3", picked3)
-        result_early = sb.tile([P, early], F32, name="result_early", align_bytes=64)
-        nc.vector.scalar_tensor_tensor(
-            result_early[:], read_early[:], gate[:], kept_part[:, 0:early], ALU.mult, ALU.add
-        )
-        nc.sync.dma_start(out[:, 0:early], result_early[:])
-
-        val_q.append(quantise("val3", grouped3))
-        read_late = ps.tile([P, P], F32, name="read_late")
-        read(read_late[:], BLOCKS - 1)
-        result_late = sb.tile([P, P], F32, name="result_late", align_bytes=64)
-        nc.vector.scalar_tensor_tensor(
-            result_late[:], read_late[:], gate[:], kept_part[:, early:E], ALU.mult, ALU.add
-        )
-        nc.sync.dma_start(out[:, early:E], result_late[:])
+        turn(gather_values(3), val_grouped[3][:])
+        codes, scales = quantise("val2", val_grouped[2][:], P, after_gather(3, 0, [P, P], U32, "val2_codes"))
+        read(read2[:], codes[:], scales[:])
+        finish("result01", read01[:], 0, 2 * P)
+        codes, scales = quantise("val3", val_grouped[3][:], P, sb.tile([P, P], U32, name="val3_codes", align_bytes=64))
+        read(read3[:], codes[:], scales[:])
+        finish("result2", read2[:], 2 * P, 3 * P)
+        finish("result3", read3[:], 3 * P, 4 * P)

@@ -36,27 +36,27 @@ def tile_attend_updateread_kernel(tc, query, keys_words, keys_scales, th, steep,
         key_bytes = sb.tile([P, T], U8, name="key_bytes", align_bytes=64)
         query_raw = sb.tile([P, PACK, Q], F32, name="query_raw", align_bytes=64)
         val_pool = [vp.tile([P, T], F32, name="val_pool%d" % b, offset=b * POOL_BYTES, align_bytes=64) for b in range(BLOCKS)]
-        kept_sb = sb.tile([P, E], F32, name="kept_sb", align_bytes=64)
-        th_sb = sb.tile([P, 1], F32, name="th_sb")
-        steep_sb = sb.tile([P, 1], F32, name="steep_sb")
+        kept_sb = vp.tile([P, E], F32, name="kept_sb", offset=BLOCKS * POOL_BYTES, align_bytes=64)
         size_sb = sb.tile([P, PACK], F32, name="size_sb")
+        vec_rows = sb.tile([P, P], F32, name="vec_rows", align_bytes=64)
         ident = sb.tile([P, P], F32, name="ident", align_bytes=64)
 
         nc.gpsimd.memset(key_bytes[:].bitcast(I32), 0)
-        nc.sync.dma_start(offsets[:], offs)
+        nc.gpsimd.memset(vec_rows[:], 0.0)
         nc.sync.dma_start(key_words[:].bitcast(I32), keys_words[0].bitcast(I32))
-        for quad in range(4):
+        nc.sync.dma_start(offsets[:], offs)
+        for r in range(4):
             nc.sync.dma_start(
-                key_bytes[32 * quad : 32 * quad + 4, :].bitcast(I32),
-                keys_scales[0, 4 * quad : 4 * quad + 4, :].bitcast(I32),
+                key_bytes[r:P:32, :].bitcast(I32),
+                keys_scales[0, r:16:4, :].bitcast(I32),
             )
         nc.sync.dma_start(query_raw[:], query.rearrange("(p j) q -> p j q", j=PACK))
         for b in range(BLOCKS):
             nc.sync.dma_start(val_pool[b][:], vals[b * P : (b + 1) * P, :])
             if b == 0:
                 nc.sync.dma_start(size_sb[:], size.rearrange("o (p t) -> (o p) t", t=PACK))
-                nc.sync.dma_start(steep_sb[:], steep)
-                nc.sync.dma_start(th_sb[:], th)
+                nc.sync.dma_start(vec_rows[0:1, :], steep.rearrange("q o -> o q"))
+                nc.sync.dma_start(vec_rows[1:2, :], th.rearrange("q o -> o q"))
         nc.sync.dma_start(kept_sb[:], kept)
         make_identity(nc, ident[:])
 
@@ -89,9 +89,10 @@ def tile_attend_updateread_kernel(tc, query, keys_words, keys_scales, th, steep,
         nc.vector.tensor_copy(key_bytes_picked[:], key_bytes[:].indirect(offsets[:]))
 
         query_grouped = sb.tile([P, Q * PACK], BF16, name="query_grouped", align_bytes=64)
-        nc.scalar.copy(
+        nc.scalar.activation(
             query_grouped[:].rearrange("p (q j) -> p q j", j=PACK),
             query_raw[:].rearrange("p j q -> p q j"),
+            ACT.Copy,
         )
         query_codes, query_scales = quantise(
             "query", query_grouped[:], Q, sb.tile([P, Q], U32, name="query_codes", align_bytes=64)
@@ -112,11 +113,6 @@ def tile_attend_updateread_kernel(tc, query, keys_words, keys_scales, th, steep,
         for t in range(PACK):
             nc.tensor.transpose(size_rows[:, t, :], size_sb[:, t : t + 1].to_broadcast([P, P]), ident[:])
 
-        gate_scale = sb.tile([P, 1], F32, name="gate_scale")
-        gate_bias = sb.tile([P, 1], F32, name="gate_bias")
-        nc.scalar.activation(gate_scale[:], steep_sb[:], ACT.Copy, scale=-0.5)
-        nc.scalar.activation(gate_bias[:], th_sb[:], ACT.Copy, scale=gate_scale[:])
-
         picked0 = gather_values(0)
 
         neg_best = after_gather(0, 0, [P, 1], F32, "neg_best")
@@ -127,6 +123,12 @@ def tile_attend_updateread_kernel(tc, query, keys_words, keys_scales, th, steep,
 
         grouped0 = sb.tile([P, P * PACK], BF16, name="val_grouped0", align_bytes=64)
         turn(picked0, grouped0[:])
+        vec_turned = ps.tile([P, P], F32, name="vec_turned")
+        nc.tensor.transpose(vec_turned[:], vec_rows[:], ident[:])
+        gate_scale = sb.tile([P, 1], F32, name="gate_scale")
+        gate_bias = sb.tile([P, 1], F32, name="gate_bias")
+        nc.scalar.activation(gate_scale[:], vec_turned[:, 0:1], ACT.Copy, scale=-0.5)
+        nc.scalar.activation(gate_bias[:], vec_turned[:, 1:2], ACT.Copy, scale=gate_scale[:])
         half_swing = sb.tile([P, 1], F32, name="half_swing")
         gate = sb.tile([P, 1], F32, name="gate")
         keep = sb.tile([P, 1], F32, name="keep")
@@ -152,10 +154,8 @@ def tile_attend_updateread_kernel(tc, query, keys_words, keys_scales, th, steep,
         turn(weights[:], pair_grouped[:, 0 : P * PACK])
         codes0, scales0 = quantise("val0", grouped0[:], P, after_gather(1, 64, [P, P], U32, "val0_codes"))
 
-        val_grouped = [None, None] + [
-            sb.tile([P, P * PACK], BF16, name="val_grouped%d" % b, align_bytes=64) for b in range(2, BLOCKS)
-        ]
-        turn(gather_values(2), val_grouped[2][:])
+        grouped2 = sb.tile([P, P * PACK], BF16, name="val_grouped2", align_bytes=64)
+        turn(gather_values(2), grouped2[:])
         first_codes, first_scales = quantise("pair", pair_grouped[:], 2 * P, after_gather(2, 0, [P, 2 * P], U32, "pair_codes"))
 
         def read(bank, codes, scales):
@@ -182,11 +182,12 @@ def tile_attend_updateread_kernel(tc, query, keys_words, keys_scales, th, steep,
         read(read01[:, 0:P], codes0[:], scales0[:])
         read(read01[:, P : 2 * P], first_codes[:, P : 2 * P], first_scales[:, P : 2 * P])
         nc.scalar.activation(kept_part[:], kept_sb[:], ACT.Copy, scale=keep[:])
-        turn(gather_values(3), val_grouped[3][:])
-        codes, scales = quantise("val2", val_grouped[2][:], P, after_gather(3, 0, [P, P], U32, "val2_codes"))
+        grouped3 = after_gather(BLOCKS, 0, [P, P * PACK], BF16, "val_grouped3")
+        turn(gather_values(3), grouped3[:])
+        codes, scales = quantise("val2", grouped2[:], P, after_gather(3, 0, [P, P], U32, "val2_codes"))
         read(read2[:], codes[:], scales[:])
         finish("result01", read01[:], 0, 2 * P)
-        codes, scales = quantise("val3", val_grouped[3][:], P, sb.tile([P, P], U32, name="val3_codes", align_bytes=64))
+        codes, scales = quantise("val3", grouped3[:], P, sb.tile([P, P], U32, name="val3_codes", align_bytes=64))
         read(read3[:], codes[:], scales[:])
         finish("result2", read2[:], 2 * P, 3 * P)
         finish("result3", read3[:], 3 * P, 4 * P)

from contextlib import ExitStack

import concourse.mybir as mybir
from concourse.masks import make_identity

F32 = mybir.dt.float32
BF16 = mybir.dt.bfloat16
I32 = mybir.dt.int32
U32 = mybir.dt.uint32
U16 = mybir.dt.uint16
U8 = mybir.dt.uint8
FP8X4 = mybir.dt.float8_e4m3fn_x4
FP4X4 = mybir.dt.float4_e2m1fn_x4
ALU = mybir.AluOpType
ACT = mybir.ActivationFunctionType
AX = mybir.AxisListType

P = 128
D, T, SLOTS, Q, E = 512, 2048, 512, 128, 512
PACK = 4
BLOCKS = E // P
POOL_BYTES = 4 * T
FLOPS = 2 * Q * SLOTS * D + 2 * Q * SLOTS * E


def tile_attend_updateread_kernel(tc, query, keys_words, keys_scales, th, steep, kept, size, vals, offs, out):
    nc = tc.nc
    with ExitStack() as ctx:
        sb = ctx.enter_context(tc.tile_pool(name="sb", bufs=1))
        vp = ctx.enter_context(tc.tile_pool(name="vp", bufs=1))
        ps = ctx.enter_context(tc.psum_pool(name="ps", bufs=1))
        ps_turn = ctx.enter_context(tc.psum_pool(name="ps_turn", bufs=2))

        offsets = sb.tile([P, SLOTS // 16], U16, name="offsets")
        key_words = sb.tile([P, T], U16, name="key_words", align_bytes=64)
        key_bytes = sb.tile([P, T], U8, name="key_bytes", align_bytes=64)
        query_raw = sb.tile([P, PACK, Q], F32, name="query_raw", align_bytes=64)
        val_pool = [vp.tile([P, T], F32, name="val_pool%d" % b, offset=b * POOL_BYTES, align_bytes=64) for b in range(BLOCKS)]
        kept_sb = vp.tile([P, E], F32, name="kept_sb", offset=BLOCKS * POOL_BYTES, align_bytes=64)
        size_sb = sb.tile([P, PACK], F32, name="size_sb")
        vec_rows = sb.tile([P, P], F32, name="vec_rows", align_bytes=64)
        ident = sb.tile([P, P], F32, name="ident", align_bytes=64)

        nc.gpsimd.memset(key_bytes[:].bitcast(I32), 0)
        nc.gpsimd.memset(vec_rows[:], 0.0)
        nc.sync.dma_start(key_words[:].bitcast(I32), keys_words[0].bitcast(I32))
        nc.sync.dma_start(offsets[:], offs)
        for r in range(4):
            nc.sync.dma_start(
                key_bytes[r:P:32, :].bitcast(I32),
                keys_scales[0, r:16:4, :].bitcast(I32),
            )
        nc.sync.dma_start(query_raw[:], query.rearrange("(p j) q -> p j q", j=PACK))
        for b in range(BLOCKS):
            nc.sync.dma_start(val_pool[b][:], vals[b * P : (b + 1) * P, :])
            if b == 0:
                nc.sync.dma_start(size_sb[:], size.rearrange("o (p t) -> (o p) t", t=PACK))
                nc.sync.dma_start(vec_rows[0:1, :], steep.rearrange("q o -> o q"))
                nc.sync.dma_start(vec_rows[1:2, :], th.rearrange("q o -> o q"))
        nc.sync.dma_start(kept_sb[:], kept)
        make_identity(nc, ident[:])

        def after_gather(b, byte, shape, dtype, name):
            return vp.tile(shape, dtype, name=name, offset=b * POOL_BYTES + byte, align_bytes=64)

        def quantise(name, grouped, width, codes):
            scales = sb.tile([P, width], U8, name=name + "_scales", align_bytes=64)
            nc.vector.quantize_mx(out=codes[:].bitcast(FP8X4), scales=scales[:], in_=grouped)
            return codes, scales

        def turn(rows, grouped):
            words = rows.bitcast(F32)
            turned = ps_turn.tile([P, 2, P], F32, name="turned")
            for u in range(2):
                nc.tensor.transpose(turned[:, u, :], words[:, u : SLOTS // 2 : 2], ident[:])
            nc.scalar.copy(
                grouped.bitcast(F32).rearrange("p (c u) -> p c u", u=2),
                turned[:].rearrange("p u c -> p c u"),
            )

        def gather_values(b):
            picked = sb.tile([P, SLOTS], BF16, name="val_picked%d" % b, align_bytes=64)
            nc.vector.tensor_copy(picked[:], val_pool[b][:].indirect(offsets[:]))
            return picked[:]

        key_words_picked = sb.tile([P, SLOTS], U16, name="key_words_picked", align_bytes=64)
        key_bytes_picked = sb.tile([P, SLOTS], U8, name="key_bytes_picked", align_bytes=64)
        nc.vector.tensor_copy(key_words_picked[:], key_words[:].indirect(offsets[:]))
        nc.vector.tensor_copy(key_bytes_picked[:], key_bytes[:].indirect(offsets[:]))

        query_grouped = sb.tile([P, Q * PACK], BF16, name="query_grouped", align_bytes=64)
        nc.scalar.activation(
            query_grouped[:].rearrange("p (q j) -> p q j", j=PACK),
            query_raw[:].rearrange("p j q -> p q j"),
            ACT.Copy,
        )
        query_codes, query_scales = quantise(
            "query", query_grouped[:], Q, sb.tile([P, Q], U32, name="query_codes", align_bytes=64)
        )

        scores = ps.tile([P, SLOTS], F32, name="scores")
        nc.tensor.matmul_mx(
            out=scores[:],
            lhsT=query_codes[:].bitcast(FP8X4),
            lhsT_scale=query_scales[:],
            rhs=key_words_picked[:].bitcast(FP4X4),
            rhs_scale=key_bytes_picked[:],
            start=True,
            stop=True,
        )

        size_rows = ps.tile([P, PACK, P], F32, name="size_rows")
        for t in range(PACK):
            nc.tensor.transpose(size_rows[:, t, :], size_sb[:, t : t + 1].to_broadcast([P, P]), ident[:])

        picked0 = gather_values(0)

        neg_best = after_gather(0, 0, [P, 1], F32, "neg_best")
        nc.vector.tensor_reduce(neg_best[:], scores[:], AX.X, ALU.max, negate=True)
        probs = sb.tile([P, SLOTS], F32, name="probs", align_bytes=64)
        total = sb.tile([P, 1], F32, name="total")
        nc.scalar.activation(probs[:], scores[:], ACT.Exp, bias=neg_best[:], accum_out=total[:])

        grouped0 = sb.tile([P, P * PACK], BF16, name="val_grouped0", align_bytes=64)
        turn(picked0, grouped0[:])
        vec_turned = ps.tile([P, P], F32, name="vec_turned")
        nc.tensor.transpose(vec_turned[:], vec_rows[:], ident[:])
        gate_scale = sb.tile([P, 1], F32, name="gate_scale")
        gate_bias = sb.tile([P, 1], F32, name="gate_bias")
        nc.scalar.activation(gate_scale[:], vec_turned[:, 0:1], ACT.Copy, scale=-0.5)
        nc.scalar.activation(gate_bias[:], vec_turned[:, 1:2], ACT.Copy, scale=gate_scale[:])
        half_swing = sb.tile([P, 1], F32, name="half_swing")
        gate = sb.tile([P, 1], F32, name="gate")
        keep = sb.tile([P, 1], F32, name="keep")
        nc.scalar.activation(half_swing[:], neg_best[:], ACT.Tanh, bias=gate_bias[:], scale=gate_scale[:])
        nc.scalar.activation(gate[:], half_swing[:], ACT.Copy, bias=0.5, scale=0.5)
        nc.scalar.activation(keep[:], half_swing[:], ACT.Copy, bias=0.5, scale=-0.5)

        picked1 = gather_values(1)
        pair_grouped = sb.tile([P, 2 * P * PACK], BF16, name="pair_grouped", align_bytes=64)
        turn(picked1, pair_grouped[:, P * PACK : 2 * P * PACK])

        inv_total = after_gather(1, 0, [P, 1], F32, "inv_total")
        nc.vector.reciprocal(inv_total[:], total[:])
        weights = sb.tile([P, SLOTS], BF16, name="weights", align_bytes=64)
        nc.vector.scalar_tensor_tensor(
            weights[:].rearrange("p (s t) -> p s t", t=PACK),
            probs[:].rearrange("p (s t) -> p s t", t=PACK),
            inv_total[:],
            size_rows[:].rearrange("p t s -> p s t"),
            ALU.mult,
            ALU.mult,
        )
        turn(weights[:], pair_grouped[:, 0 : P * PACK])
        codes0, scales0 = quantise("val0", grouped0[:], P, after_gather(1, 64, [P, P], U32, "val0_codes"))

        grouped2 = sb.tile([P, P * PACK], BF16, name="val_grouped2", align_bytes=64)
        turn(gather_values(2), grouped2[:])
        first_codes, first_scales = quantise("pair", pair_grouped[:], 2 * P, after_gather(2, 0, [P, 2 * P], U32, "pair_codes"))

        def read(bank, codes, scales):
            nc.tensor.matmul_mx(
                out=bank,
                lhsT=first_codes[:, 0:P].bitcast(FP8X4),
                lhsT_scale=first_scales[:, 0:P],
                rhs=codes.bitcast(FP8X4),
                rhs_scale=scales,
                start=True,
                stop=True,
            )

        kept_part = sb.tile([P, E], F32, name="kept_part", align_bytes=64)

        def finish(name, bank, lo, hi):
            result = sb.tile([P, hi - lo], F32, name=name, align_bytes=64)
            nc.vector.scalar_tensor_tensor(result[:], bank, gate[:], kept_part[:, lo:hi], ALU.mult, ALU.add)
            nc.sync.dma_start(out[:, lo:hi], result[:])

        read01 = ps.tile([P, 2 * P], F32, name="read01")
        read2 = ps.tile([P, P], F32, name="read2")
        read3 = ps.tile([P, P], F32, name="read3")
        read(read01[:, 0:P], codes0[:], scales0[:])
        read(read01[:, P : 2 * P], first_codes[:, P : 2 * P], first_scales[:, P : 2 * P])
        nc.scalar.activation(kept_part[:], kept_sb[:], ACT.Copy, scale=keep[:])
        grouped3 = after_gather(BLOCKS, 0, [P, P * PACK], BF16, "val_grouped3")
        turn(gather_values(3), grouped3[:])
        codes, scales = quantise("val2", grouped2[:], P, after_gather(3, 0, [P, P], U32, "val2_codes"))
        read(read2[:], codes[:], scales[:])
        finish("result01", read01[:], 0, 2 * P)
        codes, scales = quantise("val3", grouped3[:], P, sb.tile([P, P], U32, name="val3_codes", align_bytes=64))
        read(read3[:], codes[:], scales[:])
        finish("result2", read2[:], 2 * P, 3 * P)
        finish("result3", read3[:], 3 * P, 4 * P)
